import numpy as np, ml_dtypes
CORES = [52,68,84,180,196,212,308,324,340]
N = 9
T, CAP = 1024, 128
def entries(a): return a.T.reshape(-1)
def pack(v, P): return np.ascontiguousarray(np.asarray(v, np.int32).reshape(-1, P).T)
def lists(rng, how):
    n = rng.integers(0, CAP + 1, (N, 8))
    if how in ("comb", "full"): n[:] = CAP
    if how == "one": n[:] = 1
    if how == "none": n[int(rng.integers(N))] = 0; n[:, int(rng.integers(8))] = 0
    F = np.zeros((N, 8, T), np.int64)
    for r in range(N):
        for h in range(8):
            o = (rng.permutation(16)[:, None] + 16 * np.arange(T // 16)).reshape(-1) if how == "comb" else rng.permutation(T)
            F[r, h, o[:n[r, h]]] = 1
    if how == "run":
        p = rng.permutation(8); n[:, p[:2]] = CAP; n[:, p[2]] = CAP * rng.permutation(np.arange(N) % 2); n[:, p[3]] = 0
        s = rng.integers(0, T - n + 1); s[:, p[0]] = 0; s[:, p[1]] = T - CAP; s[:, p[2]] = 16 * rng.integers(0, max(1, (T - CAP) // 16), N) + 1
        F = ((np.arange(T) >= s[:, :, None]) & (np.arange(T) < (s + n)[:, :, None])).astype(np.int64)
    return {"keep": np.stack([np.concatenate([pack(F[r, h], 16) for h in range(8)], axis=0) for r in range(N)])}
def setup_inputs(rng):
    return dict({"x": rng.standard_normal((N, 128, T), dtype=np.float32).astype(ml_dtypes.bfloat16)}, **lists(rng, "uniform"))
def setup_inputs_comb(rng):
    d = setup_inputs(rng); d.update(lists(rng, "comb"))
    for k in ("x",): d[k] = (d[k].astype(np.float32) * 1048576.0).astype(d[k].dtype)
    return d
def setup_inputs_full(rng):
    d = setup_inputs(rng); d.update(lists(rng, "full"))
    for k in ("x",): d[k] = (d[k].astype(np.float32) * (1 / 1024.0)).astype(d[k].dtype)
    return d
def setup_inputs_none(rng):
    d = setup_inputs(rng); d.update(lists(rng, "none"))
    return d
def setup_inputs_one(rng):
    d = setup_inputs(rng); d.update(lists(rng, "one"))
    return d
def setup_inputs_run(rng):
    d = setup_inputs(rng); d.update(lists(rng, "run"))
    return d
def check_inputs(x):
    bad = []
    if x["keep"].min() < 0 or x["keep"].max() >= 2: bad.append("keep out of range")
    if max(int(a[16 * h:16 * h + 16].sum()) for a in x["keep"] for h in range(8)) > CAP: bad.append("a head keeps more than CAP columns on a rank")
    return bad
def reference(x, keep):
    y = np.zeros((128, N * CAP), x.dtype)
    for h in range(8):
        H = slice(16 * h, 16 * h + 16); got = np.concatenate([x[r][H][:, entries(keep[r][H]) > 0] for r in range(N)], axis=1); y[H, :got.shape[1]] = got
    return {"y": np.broadcast_to(y, (N, 128, N * CAP))}

@@ -1,0 +1,260 @@
+from concourse.bass import DstId, RemoteDMATransfer
+from concourse.mybir import AluOpType as Op, ActivationFunctionType as Act
+
+N = 9
+CAP = 128
+W = 136
+K = N * CAP // 16
+END = N * W
+PIECES = [("V", 0, 20), ("S", 36, 56), ("V", 20, 36), ("S", 56, 72)]
+
+SCRATCH = {
+    "kb": ("sbuf", [128, 64], "int32"),
+    "xs": ("sbuf", [128, 1032], "bfloat16"),
+    "land": ("sbuf", [128, END + 8], "bfloat16"),
+    "ysb": ("sbuf", [128, N * CAP], "bfloat16"),
+    "hcnt": ("sbuf", [128, 2], "bfloat16"),
+    "hdat": ("sbuf", [128, CAP], "bfloat16"),
+    "pint": ("sbuf", [128, 4], "int32"),
+    "pi2": ("sbuf", [128, 6], "int32"),
+    "pf": ("sbuf", [128, 7], "float32"),
+    "ones": ("sbuf", [128, 72], "bfloat16"),
+    "jblk": ("sbuf", [128, 128], "bfloat16"),
+    "jrow": ("sbuf", [128, 128], "bfloat16"),
+    "jmod": ("sbuf", [128, 128], "bfloat16"),
+    "k16": ("sbuf", [128, 72], "bfloat16"),
+    "k16f": ("sbuf", [128, 72], "float32"),
+    "bo": ("sbuf", [128, 128], "bfloat16"),
+    "lt": ("sbuf", [128, 128], "bfloat16"),
+    "ng": ("sbuf", [128, 128], "bfloat16"),
+    "hold": ("sbuf", [128, 128], "bfloat16"),
+    "selq": ("sbuf", [128, 512], "bfloat16"),
+    "ident": ("sbuf", [128, 128], "bfloat16"),
+    "pm": ("sbuf", [128, 72], "bfloat16"),
+    "F": ("sbuf", [128, 64], "bfloat16"),
+    "S": ("sbuf", [128, 64], "bfloat16"),
+    "Z": ("sbuf", [128, 512], "bfloat16"),
+    "Z2": ("sbuf", [128, 128], "bfloat16"),
+    "cw": ("sbuf", [128, 72], "bfloat16"),
+    "h1": ("sbuf", [128, 128], "float32"),
+    "h2": ("sbuf", [128, 128], "float32"),
+    "cl": ("sbuf", [128, 8], "uint16"),
+    "tl": ("sbuf", [128, 8], "uint16"),
+    "off": ("sbuf", [128, N], "float32"),
+    "dd": ("sbuf", [128, N], "float32"),
+    "pos": ("sbuf", [128, 72], "float32"),
+    "mr": ("sbuf", [128, N * 72], "bfloat16"),
+    "lst": ("sbuf", [128, 72], "uint16"),
+    "pcum": ("psum", [128, 512], "float32"),
+    "pb": ("psum", [128, 512], "float32"),
+    "ptot": ("psum", [128, 512], "float32"),
+    "pc": ("psum", [128, 512], "float32"),
+    "pt": ("psum", [128, 512], "float32"),
+    "pl": ("psum", [128, 512], "float32"),
+}
+SEMAPHORES = (["dir", "rcnt", "rdat", "hc", "hd", "loc", "ldk", "ldx", "i0", "i1", "i2", "i3", "i4", "mem", "pi", "pfs",
+               "sbo", "slt", "sng", "ssel", "shd", "sF", "sS", "sbp", "stot", "scum", "sc1", "sh1", "scl", "scw", "sz2",
+               "st1", "sh2", "stl", "sga", "scn", "sid", "spm", "sps", "soff", "slp", "sls", "sty", "sts"]
+              + ["z%d" % q for q in range(4)] + ["m%d" % r for r in range(N)] + ["g%d" % k for k in range(4)])
+
+
+def relay_of(T, topo, src, dsts):
+    for h in range(4 * 128):
+        if (T.rank_of(h) is None and topo.chip(h) == topo.chip(src) and topo.die(h) == topo.die(src)
+                and topo.rack(topo.host(h)) != topo.rack(topo.host(src))
+                and topo.may_write(src, h) and all(topo.same_plane(h, d) and topo.may_write(h, d) for d in dsts)):
+            return h
+    return None
+
+
+def plan(T, topo):
+    out = []
+    for s in T.cores:
+        direct = [d for d in T.cores if d != s and topo.may_write(s, d)]
+        direct.sort(key=lambda d: topo.rack(topo.host(d)) == topo.rack(topo.host(s)))
+        far = [d for d in T.cores if d != s and not topo.may_write(s, d)]
+        out.append((direct, far, relay_of(T, topo, s, far) if far else None))
+    return out
+
+
+def send(g, topo, core, dsts, src, dst, rsem, lsem):
+    m = topo.mask(core, dsts[0])
+    for d in dsts[1:]:
+        m &= topo.mask(core, d)
+    ids = []
+    for d in dsts:
+        rid, pid = topo.addr(d, core)
+        ids.append(DstId(rid=rid, pnc=pid))
+    g.remote_dma_fused([RemoteDMATransfer(dst_ids=ids, dma_engine_mask=m, remote_sem=rsem, srcs=[src],
+                                          dsts=[dst for _ in dsts])], local_sem=lsem)
+    return bin(m).count("1")
+
+
+def engines(topo, a, dsts):
+    m = topo.mask(a, dsts[0])
+    for d in dsts[1:]:
+        m &= topo.mask(a, d)
+    return bin(m).count("1")
+
+
+def relay_program(g, core, T, topo, rank, src, far):
+    sem = T.sem
+    lo = rank * W
+    n_in = engines(topo, src, [core])
+    g.wait_ge(sem.hc, n_in)
+    n = send(g, topo, core, far, T.hcnt[:], T.land[:, lo + CAP:lo + CAP + 2], sem.rcnt, sem.loc)
+    g.wait_ge(sem.hd, n_in)
+    n += send(g, topo, core, far, T.hdat[:], T.land[:, lo:lo + CAP], sem.rdat, sem.loc)
+    g.wait_ge(sem.loc, n)
+
+
+def rank_program(g, core, T, topo):
+    routes = plan(T, topo)
+    rank = T.rank_of(core)
+    if rank is None:
+        for r, (direct, far, relay) in enumerate(routes):
+            if relay == core:
+                relay_program(g, core, T, topo, r, T.cores[r], far)
+        return
+    V, P, A, Y, sem = g.vector, g.tensor, g.scalar, g.sync, T.sem
+    direct, far, relay = routes[rank]
+    lo = rank * W
+
+    n_dir = sum(engines(topo, T.cores[r], routes[r][0]) for r in range(N) if core in routes[r][0])
+    n_rel = sum(engines(topo, routes[r][2], routes[r][1]) for r in range(N) if core in routes[r][1])
+
+    Y.dma_start(T.kb[:], T.keep[:]).then_inc(sem.ldk, 16)
+    Y.dma_start(T.xs[:, 0:1024], T.x[:]).then_inc(sem.ldx, 16)
+
+    g.iota(T.pint[:], [[128, 4]], 0, 1).then_inc(sem.i0, 1)
+    g.iota(T.jblk[:], [[1, 8], [0, 16]], 0, 0, allow_small_or_imprecise_dtypes=True).then_inc(sem.i1, 1)
+    g.iota(T.jrow[:], [[1, 128]], 0, 0, allow_small_or_imprecise_dtypes=True).then_inc(sem.i2, 1)
+    g.iota(T.jmod[:], [[0, 8], [1, 16]], 0, 0, allow_small_or_imprecise_dtypes=True).then_inc(sem.i3, 1)
+    g.iota(T.k16f[:], [[16, K]], 0, 0, allow_small_or_imprecise_dtypes=True).then_inc(sem.i4, 1)
+    n_loc = 0
+    g.wait_ge(sem.scn, 1)
+    if far:
+        n_loc += send(g, topo, core, [relay], T.land[:, lo + CAP:lo + CAP + 2], T.hcnt[:], sem.hc, sem.loc)
+    g.wait_ge(sem.sga, 1)
+    if far:
+        n_loc += send(g, topo, core, [relay], T.land[:, lo:lo + CAP], T.hdat[:], sem.hd, sem.loc)
+    n_loc += send(g, topo, core, direct, T.land[:, lo:lo + CAP + 2], T.land[:, lo:lo + CAP + 2], sem.dir, sem.loc)
+    g.wait_ge(sem.loc, n_loc)
+
+    V.memset(T.ones[:], 1.0).then_inc(sem.mem, 1)
+    V.memset(T.xs[:, 1024:1032], 0.0).then_inc(sem.mem, 1)
+    V.memset(T.cw[:, 64:72], 1000.0).then_inc(sem.mem, 1)
+    V.memset(T.land[:, END:END + 8], 0.0).then_inc(sem.mem, 1)
+    V.wait_ge(sem.i0, 1)
+    V.tensor_scalar(T.pi2[:, 0:4], T.pint[:], 6, None, Op.arith_shift_right).then_inc(sem.pi, 1)
+    V.tensor_scalar(T.pi2[:, 4:5], T.pint[:, 0:1], 4, None, Op.arith_shift_right).then_inc(sem.pi, 1)
+    V.tensor_scalar(T.pi2[:, 5:6], T.pint[:, 0:1], 15, None, Op.bitwise_and).then_inc(sem.pi, 1)
+    V.tensor_copy(T.pf[:, 6:7], T.pint[:, 0:1]).then_inc(sem.pfs, 1)
+    V.wait_ge(sem.pi, 3)
+    V.tensor_copy(T.pf[:, 0:6], T.pi2[:]).then_inc(sem.pfs, 1)
+    V.wait_ge(sem.pfs, 2)
+    V.wait_ge(sem.i1, 1)
+    V.tensor_scalar(T.bo[:], T.jblk[:], T.pf[:, 4:5], None, Op.is_equal).then_inc(sem.sbo, 1)
+    for q in range(4):
+        V.tensor_scalar(T.selq[:, 128 * q:128 * q + 128], T.jblk[:], T.pf[:, q:q + 1], 16.0, Op.is_equal, Op.mult).then_inc(sem.ssel, 1)
+    V.wait_ge(sem.i2, 1)
+    V.tensor_scalar(T.lt[:], T.jrow[:], T.pf[:, 6:7], -1.0, Op.is_lt, Op.mult).then_inc(sem.slt, 1)
+    V.wait_ge(sem.sbo, 1)
+    V.wait_ge(sem.slt, 1)
+    V.tensor_tensor(T.ng[:], T.bo[:], T.lt[:], Op.mult).then_inc(sem.sng, 1)
+    V.wait_ge(sem.i3, 1)
+    V.tensor_scalar(T.hold[:], T.jmod[:], T.pf[:, 5:6], 4096.0, Op.is_equal, Op.mult).then_inc(sem.shd, 1)
+
+    V.wait_ge(sem.mem, 4)
+    V.wait_ge(sem.ldk, 16)
+    V.tensor_copy(T.F[:], T.kb[:]).then_inc(sem.sF, 1)
+    V.wait_ge(sem.sF, 1)
+    V.tensor_tensor_scan(T.S[:], T.ones[:, 0:64], T.F[:], 0.0, Op.mult, Op.add).then_inc(sem.sS, 1)
+    V.wait_ge(sem.sbp, 2)
+    for q in range(4):
+        V.tensor_scalar(T.Z[:, 128 * q:128 * q + 128], T.jrow[:], T.pb[:, q:q + 1], None, Op.is_ge).then_inc(sem["z%d" % q], 1)
+    V.wait_ge(sem.shd, 1)
+    V.wait_ge(sem.sc1, 1)
+    V.tensor_tensor_scan(T.h1[:], T.hold[:], T.pc[:, 0:128], 0.0, Op.add, Op.min).then_inc(sem.sh1, 1)
+    V.wait_ge(sem.sh1, 1)
+    V.tensor_scalar(T.cl[:], T.h1[:, 15:128:16], 0.0625, None, Op.mult).then_inc(sem.scl, 1)
+    V.wait_ge(sem.scl, 1)
+    V.wait_ge(sem.scw, 1)
+    V.tensor_tensor(T.Z2[:], T.cw[:, 0:65].indirect(T.cl[:, 0:8]), T.jrow[:], Op.is_le).then_inc(sem.sz2, 1)
+    V.wait_ge(sem.st1, 1)
+    V.tensor_tensor_scan(T.h2[:], T.hold[:], T.pt[:, 0:128], 0.0, Op.add, Op.min).then_inc(sem.sh2, 1)
+    V.wait_ge(sem.sh2, 1)
+    V.tensor_copy(T.tl[:], T.h2[:, 15:128:16]).then_inc(sem.stl, 1)
+    V.wait_ge(sem.stl, 1)
+    V.wait_ge(sem.ldx, 16)
+    V.tensor_copy(T.land[:, lo:lo + CAP], T.xs[:, 0:1025].indirect(T.tl[:, 0:8])).then_inc(sem.sga, 1)
+
+    P.wait_ge(sem.sbo, 1)
+    P.wait_ge(sem.sng, 1)
+    P.wait_ge(sem.sF, 1)
+    P.matmul(T.pcum[:, 0:64], T.ng[:], T.F[:], True, False)
+    P.wait_ge(sem.sS, 1)
+    P.matmul(T.pb[0:64, 0:4], T.S[:], T.bo[:, 0:128:32], True, True).then_inc(sem.sbp, 1)
+    P.matmul(T.pb[64:128, 0:4], T.S[:], T.bo[:, 16:128:32], True, True).then_inc(sem.sbp, 1)
+    P.matmul(T.ptot[:, 0:2], T.bo[:], T.S[:, 62:64], True, True).then_inc(sem.stot, 1)
+    P.matmul(T.pcum[:, 0:64], T.bo[:], T.S[:], False, True).then_inc(sem.scum, 1)
+    P.wait_ge(sem.ssel, 4)
+    for q in range(4):
+        P.wait_ge(sem["z%d" % q], 1)
+        mm = P.matmul(T.pc[:, 0:128], T.selq[:, 128 * q:128 * q + 128], T.Z[:, 128 * q:128 * q + 128], q == 0, q == 3)
+    mm.then_inc(sem.sc1, 1)
+    for q in range(4):
+        P.matmul(T.pt[:, 0:128], T.selq[:, 128 * q:128 * q + 128], T.Z[:, 128 * q:128 * q + 128], q == 0, False)
+    P.wait_ge(sem.sz2, 1)
+    P.matmul(T.pt[:, 0:128], T.bo[:], T.Z2[:], False, True).then_inc(sem.st1, 1)
+
+    A.wait_ge(sem.stot, 1)
+    A.activation(T.land[:, lo + CAP:lo + CAP + 2], T.ptot[:, 0:2], Act.Copy).then_inc(sem.scn, 1)
+    A.wait_ge(sem.scum, 1)
+    A.activation(T.cw[:, 0:64], T.pcum[:, 0:64], Act.Copy).then_inc(sem.scw, 1)
+
+    V.tensor_scalar(T.ident[:], T.jrow[:], T.pf[:, 6:7], None, Op.is_equal).then_inc(sem.sid, 1)
+    V.wait_ge(sem.i4, 1)
+    V.tensor_scalar(T.pos[:], T.k16f[:], T.pf[:, 5:6], None, Op.add).then_inc(sem.sps, 1)
+    V.tensor_copy(T.k16[:], T.k16f[:]).then_inc(sem.spm, 1)
+    V.tensor_scalar(T.pm[:], T.ones[:], T.pf[:, 5:6], None, Op.mult).then_inc(sem.spm, 1)
+    P.wait_ge(sem.sid, 1)
+    P.wait_ge(sem.spm, 2)
+    P.matmul(T.pl[:, 0:K], T.ident[:], T.k16[:], True, False)
+    P.matmul(T.pl[:, 0:K], T.ident[:], T.pm[:], False, False)
+    V.wait_ge(sem.sps, 1)
+    V.wait_ge(sem.scn, 1)
+    V.wait_ge(sem.dir, n_dir)
+    if n_rel:
+        V.wait_ge(sem.rcnt, n_rel)
+    cnts = T.land[:, CAP + 1:END:W]
+    V.tensor_tensor_scan(T.off[:], T.ones[:, 0:N], cnts, 0.0, Op.mult, Op.add).then_inc(sem.soff, 1)
+    V.tensor_scalar(T.dd[:], cnts, -1.0, float(W), Op.mult, Op.add).then_inc(sem.soff, 1)
+    V.wait_ge(sem.soff, 2)
+    for r in range(N):
+        V.tensor_scalar(T.mr[:, K * r:K * r + K], T.pos[:], T.off[:, r:r + 1], T.dd[:, r:r + 1], Op.is_ge, Op.mult).then_inc(sem["m%d" % r], 1)
+        P.wait_ge(sem["m%d" % r], 1)
+        mm = P.matmul(T.pl[:, 0:K], T.ident[:], T.mr[:, K * r:K * r + K], False, r == N - 1)
+    mm.then_inc(sem.slp, 1)
+    V.wait_ge(sem.slp, 1)
+    V.tensor_scalar(T.lst[:], T.pl[:, 0:K], float(END), None, Op.min).then_inc(sem.sls, 1)
+
+    V.wait_ge(sem.sls, 1)
+    A.wait_ge(sem.sls, 1)
+    if n_rel:
+        V.wait_ge(sem.rdat, n_rel)
+        A.wait_ge(sem.rdat, n_rel)
+    for k, (who, a, b) in enumerate(PIECES):
+        win = T.land[:, 0:END + 1].indirect(T.lst[:, a:b])
+        if who == "V":
+            V.tensor_copy(T.ysb[:, 16 * a:16 * b], win).then_inc(sem["g%d" % k], 1)
+        else:
+            A.activation(T.ysb[:, 16 * a:16 * b], win, Act.Copy).then_inc(sem["g%d" % k], 1)
+    for k, (who, a, b) in enumerate(PIECES[:3]):
+        Y.wait_ge(sem["g%d" % k], 1)
+        Y.dma_start(T.y[:, 16 * a:16 * b], T.ysb[:, 16 * a:16 * b]).then_inc(sem.sty, 16)
+    a, b = PIECES[3][1:]
+    A.wait_ge(sem.g3, 1)
+    A.dma_start(T.y[:, 16 * a:16 * b], T.ysb[:, 16 * a:16 * b]).then_inc(sem.sts, 16)
+    Y.wait_ge(sem.sty, 48)
+    A.wait_ge(sem.sts, 16)

@@ -1,110 +1,79 @@
 from concourse.bass import DstId, RemoteDMATransfer
 from concourse.mybir import AluOpType as Op, ActivationFunctionType as Act
 
-N = 9
-CAP = 128
+N, CAP = 9, 128
 W = 136
 K = N * CAP // 16
 END = N * W
 PIECES = [("V", 0, 20), ("S", 36, 56), ("V", 20, 36), ("S", 56, 72)]
 
-SCRATCH = {
-    "kb": ("sbuf", [128, 64], "int32"),
-    "xs": ("sbuf", [128, 1032], "bfloat16"),
-    "land": ("sbuf", [128, END + 8], "bfloat16"),
-    "ysb": ("sbuf", [128, N * CAP], "bfloat16"),
-    "hcnt": ("sbuf", [128, 2], "bfloat16"),
-    "hdat": ("sbuf", [128, CAP], "bfloat16"),
-    "pint": ("sbuf", [128, 4], "int32"),
-    "pi2": ("sbuf", [128, 6], "int32"),
-    "pf": ("sbuf", [128, 7], "float32"),
-    "ones": ("sbuf", [128, 72], "bfloat16"),
-    "jblk": ("sbuf", [128, 128], "bfloat16"),
-    "jrow": ("sbuf", [128, 128], "bfloat16"),
-    "jmod": ("sbuf", [128, 128], "bfloat16"),
-    "k16": ("sbuf", [128, 72], "bfloat16"),
-    "k16f": ("sbuf", [128, 72], "float32"),
-    "bo": ("sbuf", [128, 128], "bfloat16"),
-    "lt": ("sbuf", [128, 128], "bfloat16"),
-    "ng": ("sbuf", [128, 128], "bfloat16"),
-    "hold": ("sbuf", [128, 128], "bfloat16"),
-    "selq": ("sbuf", [128, 512], "bfloat16"),
-    "ident": ("sbuf", [128, 128], "bfloat16"),
-    "pm": ("sbuf", [128, 72], "bfloat16"),
-    "F": ("sbuf", [128, 64], "bfloat16"),
-    "S": ("sbuf", [128, 64], "bfloat16"),
-    "Z": ("sbuf", [128, 512], "bfloat16"),
-    "Z2": ("sbuf", [128, 128], "bfloat16"),
-    "cw": ("sbuf", [128, 72], "bfloat16"),
-    "h1": ("sbuf", [128, 128], "float32"),
-    "h2": ("sbuf", [128, 128], "float32"),
-    "cl": ("sbuf", [128, 8], "uint16"),
-    "tl": ("sbuf", [128, 8], "uint16"),
-    "off": ("sbuf", [128, N], "float32"),
-    "dd": ("sbuf", [128, N], "float32"),
-    "pos": ("sbuf", [128, 72], "float32"),
-    "mr": ("sbuf", [128, N * 72], "bfloat16"),
-    "lst": ("sbuf", [128, 72], "uint16"),
-    "pcum": ("psum", [128, 512], "float32"),
-    "pb": ("psum", [128, 512], "float32"),
-    "ptot": ("psum", [128, 512], "float32"),
-    "pc": ("psum", [128, 512], "float32"),
-    "pt": ("psum", [128, 512], "float32"),
-    "pl": ("psum", [128, 512], "float32"),
-}
+BF, F32, I32, U16 = "bfloat16", "float32", "int32", "uint16"
+SB = {"kb": (64, I32), "xs": (1032, BF), "land": (END + 8, BF), "ysb": (N * CAP, BF), "hcnt": (2, BF), "hdat": (CAP, BF),
+      "pint": (4, I32), "pi2": (6, I32), "pf": (7, F32), "ones": (72, BF), "jblk": (128, BF), "jrow": (128, BF),
+      "jmod": (128, BF), "k16": (72, BF), "k16f": (72, F32), "bo": (128, BF), "lt": (128, BF), "ng": (128, BF),
+      "hold": (128, BF), "selq": (512, BF), "ident": (128, BF), "pm": (72, BF), "F": (64, BF), "S": (64, BF), "Z": (512, BF),
+      "Z2": (128, BF), "cw": (72, BF), "h1": (128, F32), "h2": (128, F32), "cl": (8, U16), "tl": (8, U16), "off": (N, F32),
+      "dd": (N, F32), "pos": (72, F32), "mr": (N * 72, BF), "lst": (72, U16)}
+SCRATCH = {k: ("sbuf", [128, n], t) for k, (n, t) in SB.items()}
+for _k in ("pcum", "pb", "ptot", "pc", "pt", "pl"):
+    SCRATCH[_k] = ("psum", [128, 512], F32)
 SEMAPHORES = (["dir", "rcnt", "rdat", "hc", "hd", "loc", "ldk", "ldx", "i0", "i1", "i2", "i3", "i4", "mem", "pi", "pfs",
                "sbo", "slt", "sng", "ssel", "shd", "sF", "sS", "sbp", "stot", "scum", "sc1", "sh1", "scl", "scw", "sz2",
                "st1", "sh2", "stl", "sga", "scn", "sid", "spm", "sps", "soff", "slp", "sls", "sty", "sts"]
               + ["z%d" % q for q in range(4)] + ["m%d" % r for r in range(N)] + ["g%d" % k for k in range(4)])
 
 
-def relay_of(T, topo, src, dsts):
-    for h in range(4 * 128):
-        if (T.rank_of(h) is None and topo.chip(h) == topo.chip(src) and topo.die(h) == topo.die(src)
-                and topo.rack(topo.host(h)) != topo.rack(topo.host(src))
-                and topo.may_write(src, h) and all(topo.same_plane(h, d) and topo.may_write(h, d) for d in dsts)):
-            return h
-    return None
-
-
 def plan(T, topo):
-    out = []
+    used, out = set(), []
+    hosts = sorted(set(topo.host(c) for c in T.cores))
     for s in T.cores:
-        direct = [d for d in T.cores if d != s and topo.may_write(s, d)]
-        direct.sort(key=lambda d: topo.rack(topo.host(d)) == topo.rack(topo.host(s)))
-        far = [d for d in T.cores if d != s and not topo.may_write(s, d)]
-        out.append((direct, far, relay_of(T, topo, s, far) if far else None))
+        direct = [d for d in T.cores if d != s and topo.same_plane(s, d)]
+        relays = []
+        for hh in hosts:
+            dsts = [d for d in T.cores if topo.host(d) == hh]
+            if topo.rack(hh) == topo.rack(topo.host(s)):
+                continue
+            for h in range(4 * 128):
+                if (T.rank_of(h) is None and h not in used and topo.chip(h) == topo.chip(s) and topo.die(h) == topo.die(s)
+                        and topo.rack(topo.host(h)) == topo.rack(hh) and topo.may_write(s, h)
+                        and all(topo.same_plane(h, d) or (topo.host(h), topo.chip(h)) == (hh, topo.chip(d)) for d in dsts)):
+                    dsts.sort(key=lambda d: not topo.same_plane(h, d))
+                    relays.append((h, dsts))
+                    used.add(h)
+                    break
+        out.append((direct, relays))
     return out
-
-
-def send(g, topo, core, dsts, src, dst, rsem, lsem):
-    m = topo.mask(core, dsts[0])
-    for d in dsts[1:]:
-        m &= topo.mask(core, d)
-    ids = []
-    for d in dsts:
-        rid, pid = topo.addr(d, core)
-        ids.append(DstId(rid=rid, pnc=pid))
-    g.remote_dma_fused([RemoteDMATransfer(dst_ids=ids, dma_engine_mask=m, remote_sem=rsem, srcs=[src],
-                                          dsts=[dst for _ in dsts])], local_sem=lsem)
-    return bin(m).count("1")
 
 
 def engines(topo, a, dsts):
     m = topo.mask(a, dsts[0])
     for d in dsts[1:]:
         m &= topo.mask(a, d)
+    return m
+
+
+def count(m):
     return bin(m).count("1")
 
 
-def relay_program(g, core, T, topo, rank, src, far):
+def send(g, topo, core, dsts, src, dst, rsem, lsem):
+    m = engines(topo, core, dsts)
+    ids = []
+    for d in dsts:
+        rid, pid = topo.addr(d, core)
+        ids.append(DstId(rid=rid, pnc=pid))
+    g.remote_dma_fused([RemoteDMATransfer(dst_ids=ids, dma_engine_mask=m, remote_sem=rsem, srcs=[src],
+                                          dsts=[dst for _ in dsts])], local_sem=lsem)
+    return count(m)
+
+
+def relay_program(g, core, T, topo, rank, n_in, dsts):
     sem = T.sem
     lo = rank * W
-    n_in = engines(topo, src, [core])
     g.wait_ge(sem.hc, n_in)
-    n = send(g, topo, core, far, T.hcnt[:], T.land[:, lo + CAP:lo + CAP + 2], sem.rcnt, sem.loc)
+    n = send(g, topo, core, dsts, T.hcnt[:], T.land[:, lo + CAP:lo + CAP + 2], sem.rcnt, sem.loc)
     g.wait_ge(sem.hd, n_in)
-    n += send(g, topo, core, far, T.hdat[:], T.land[:, lo:lo + CAP], sem.rdat, sem.loc)
+    n += send(g, topo, core, dsts, T.hdat[:], T.land[:, lo:lo + CAP], sem.rdat, sem.loc)
     g.wait_ge(sem.loc, n)
 
 
@@ -112,32 +81,32 @@ def rank_program(g, core, T, topo):
     routes = plan(T, topo)
     rank = T.rank_of(core)
     if rank is None:
-        for r, (direct, far, relay) in enumerate(routes):
-            if relay == core:
-                relay_program(g, core, T, topo, r, T.cores[r], far)
+        for r, (direct, relays) in enumerate(routes):
+            for h, dsts in relays:
+                if h == core:
+                    relay_program(g, core, T, topo, r, count(engines(topo, T.cores[r], [k for k, _ in relays])), dsts)
         return
     V, P, A, Y, sem = g.vector, g.tensor, g.scalar, g.sync, T.sem
-    direct, far, relay = routes[rank]
+    direct, relays = routes[rank]
     lo = rank * W
+    loose = {"allow_small_or_imprecise_dtypes": True}
 
-    n_dir = sum(engines(topo, T.cores[r], routes[r][0]) for r in range(N) if core in routes[r][0])
-    n_rel = sum(engines(topo, routes[r][2], routes[r][1]) for r in range(N) if core in routes[r][1])
+    n_dir = sum(count(engines(topo, T.cores[r], routes[r][0])) for r in range(N) if core in routes[r][0])
+    n_rel = sum(count(engines(topo, h, dsts)) for _, rel in routes for h, dsts in rel if core in dsts)
 
     Y.dma_start(T.kb[:], T.keep[:]).then_inc(sem.ldk, 16)
     Y.dma_start(T.xs[:, 0:1024], T.x[:]).then_inc(sem.ldx, 16)
 
     g.iota(T.pint[:], [[128, 4]], 0, 1).then_inc(sem.i0, 1)
-    g.iota(T.jblk[:], [[1, 8], [0, 16]], 0, 0, allow_small_or_imprecise_dtypes=True).then_inc(sem.i1, 1)
-    g.iota(T.jrow[:], [[1, 128]], 0, 0, allow_small_or_imprecise_dtypes=True).then_inc(sem.i2, 1)
-    g.iota(T.jmod[:], [[0, 8], [1, 16]], 0, 0, allow_small_or_imprecise_dtypes=True).then_inc(sem.i3, 1)
-    g.iota(T.k16f[:], [[16, K]], 0, 0, allow_small_or_imprecise_dtypes=True).then_inc(sem.i4, 1)
-    n_loc = 0
+    g.iota(T.jblk[:], [[1, 8], [0, 16]], 0, 0, **loose).then_inc(sem.i1, 1)
+    g.iota(T.jrow[:], [[1, 128]], 0, 0, **loose).then_inc(sem.i2, 1)
+    g.iota(T.jmod[:], [[0, 8], [1, 16]], 0, 0, **loose).then_inc(sem.i3, 1)
+    g.iota(T.k16f[:], [[16, K]], 0, 0, **loose).then_inc(sem.i4, 1)
+    hops = [h for h, _ in relays]
     g.wait_ge(sem.scn, 1)
-    if far:
-        n_loc += send(g, topo, core, [relay], T.land[:, lo + CAP:lo + CAP + 2], T.hcnt[:], sem.hc, sem.loc)
+    n_loc = send(g, topo, core, hops, T.land[:, lo + CAP:lo + CAP + 2], T.hcnt[:], sem.hc, sem.loc)
     g.wait_ge(sem.sga, 1)
-    if far:
-        n_loc += send(g, topo, core, [relay], T.land[:, lo:lo + CAP], T.hdat[:], sem.hd, sem.loc)
+    n_loc += send(g, topo, core, hops, T.land[:, lo:lo + CAP], T.hdat[:], sem.hd, sem.loc)
     n_loc += send(g, topo, core, direct, T.land[:, lo:lo + CAP + 2], T.land[:, lo:lo + CAP + 2], sem.dir, sem.loc)
     g.wait_ge(sem.loc, n_loc)
 
@@ -224,9 +193,8 @@ def rank_program(g, core, T, topo):
     P.matmul(T.pl[:, 0:K], T.ident[:], T.pm[:], False, False)
     V.wait_ge(sem.sps, 1)
     V.wait_ge(sem.scn, 1)
+    V.wait_ge(sem.rcnt, n_rel)
     V.wait_ge(sem.dir, n_dir)
-    if n_rel:
-        V.wait_ge(sem.rcnt, n_rel)
     cnts = T.land[:, CAP + 1:END:W]
     V.tensor_tensor_scan(T.off[:], T.ones[:, 0:N], cnts, 0.0, Op.mult, Op.add).then_inc(sem.soff, 1)
     V.tensor_scalar(T.dd[:], cnts, -1.0, float(W), Op.mult, Op.add).then_inc(sem.soff, 1)
@@ -241,9 +209,8 @@ def rank_program(g, core, T, topo):
 
     V.wait_ge(sem.sls, 1)
     A.wait_ge(sem.sls, 1)
-    if n_rel:
-        V.wait_ge(sem.rdat, n_rel)
-        A.wait_ge(sem.rdat, n_rel)
+    V.wait_ge(sem.rdat, n_rel)
+    A.wait_ge(sem.rdat, n_rel)
     for k, (who, a, b) in enumerate(PIECES):
         win = T.land[:, 0:END + 1].indirect(T.lst[:, a:b])
         if who == "V":

@@ -9,71 +9,116 @@ PIECES = [("V", 0, 20), ("S", 36, 56), ("V", 20, 36), ("S", 56, 72)]
 
 BF, F32, I32, U16 = "bfloat16", "float32", "int32", "uint16"
 SB = {"kb": (64, I32), "xs": (1032, BF), "land": (END + 8, BF), "ysb": (N * CAP, BF), "hcnt": (2, BF), "hdat": (CAP, BF),
-      "pint": (4, I32), "pi2": (6, I32), "pf": (7, F32), "ones": (72, BF), "jblk": (128, BF), "jrow": (128, BF),
-      "jmod": (128, BF), "k16": (72, BF), "k16f": (72, F32), "bo": (128, BF), "lt": (128, BF), "ng": (128, BF),
-      "hold": (128, BF), "selq": (512, BF), "ident": (128, BF), "pm": (72, BF), "F": (64, BF), "S": (64, BF), "Z": (512, BF),
-      "Z2": (128, BF), "cw": (72, BF), "h1": (128, F32), "h2": (128, F32), "cl": (8, U16), "tl": (8, U16), "off": (N, F32),
-      "dd": (N, F32), "pos": (72, F32), "mr": (N * 72, BF), "lst": (72, U16)}
+      "pint": (4, I32), "pi4": (4, I32), "pf": (8, F32), "bias": (4, F32), "ones": (72, BF), "U": (128, F32),
+      "jrow": (128, BF), "jmod": (128, BF), "ab": (128, BF), "al": (128, BF), "ag": (128, BF), "bo": (128, BF),
+      "le": (128, BF), "gt": (128, BF), "hold": (128, BF), "s1": (32, BF), "selw": (224, BF), "FF": (136, BF), "S": (72, BF),
+      "dm": (128, BF), "Z": (512, BF), "Z2": (128, BF), "h2": (128, F32), "tl": (8, U16), "ident": (128, BF),
+      "k16": (72, BF), "pm": (72, BF), "pos": (72, F32), "off": (N, F32), "dd": (N, F32), "mr": (N * 72, BF), "lst": (72, U16)}
 SCRATCH = {k: ("sbuf", [128, n], t) for k, (n, t) in SB.items()}
-for _k in ("pcum", "pb", "ptot", "pc", "pt", "pl"):
+for _k in ("pd", "pb", "pc", "pt", "pl", "pn"):
     SCRATCH[_k] = ("psum", [128, 512], F32)
-SEMAPHORES = (["dir", "rcnt", "rdat", "hc", "hd", "loc", "ldk", "ldx", "i0", "i1", "i2", "i3", "i4", "mem", "pi", "pfs",
-               "sbo", "slt", "sng", "ssel", "shd", "sF", "sS", "sbp", "stot", "scum", "sc1", "sh1", "scl", "scw", "sz2",
-               "st1", "sh2", "stl", "sga", "scn", "sid", "spm", "sps", "soff", "slp", "sls", "sty", "sts"]
+SEMAPHORES = (["dir", "rcnt", "rdat", "hc", "hd", "loc", "ldk", "ldx", "i0", "i1", "i2", "i3", "mem", "ph", "pp", "pi", "p2",
+               "pev", "pod", "pif", "p2f", "pfp", "bi0", "bi1", "bi2", "aab", "aal", "aag", "sbo", "sle", "sgt", "sff", "sf0",
+               "sS", "ss1", "ssw", "shd", "sbp", "spd", "sdm", "spc", "sz2", "st1", "sh2", "stl", "sga", "scn", "sid", "spm",
+               "sps", "spn", "soff", "slp", "sls", "sty", "sts"]
               + ["z%d" % q for q in range(4)] + ["m%d" % r for r in range(N)] + ["g%d" % k for k in range(4)])
-
-
-def plan(T, topo):
-    used, out = set(), []
-    hosts = sorted(set(topo.host(c) for c in T.cores))
-    for s in T.cores:
-        direct = [d for d in T.cores if d != s and topo.same_plane(s, d)]
-        relays = []
-        for hh in hosts:
-            dsts = [d for d in T.cores if topo.host(d) == hh]
-            if topo.rack(hh) == topo.rack(topo.host(s)):
-                continue
-            for h in range(4 * 128):
-                if (T.rank_of(h) is None and h not in used and topo.chip(h) == topo.chip(s) and topo.die(h) == topo.die(s)
-                        and topo.rack(topo.host(h)) == topo.rack(hh) and topo.may_write(s, h)
-                        and all(topo.same_plane(h, d) or (topo.host(h), topo.chip(h)) == (hh, topo.chip(d)) for d in dsts)):
-                    dsts.sort(key=lambda d: not topo.same_plane(h, d))
-                    relays.append((h, dsts))
-                    used.add(h)
-                    break
-        out.append((direct, relays))
-    return out
-
-
-def engines(topo, a, dsts):
-    m = topo.mask(a, dsts[0])
-    for d in dsts[1:]:
-        m &= topo.mask(a, d)
-    return m
 
 
 def count(m):
     return bin(m).count("1")
 
 
-def send(g, topo, core, dsts, src, dst, rsem, lsem):
-    m = engines(topo, core, dsts)
-    ids = []
-    for d in dsts:
-        rid, pid = topo.addr(d, core)
-        ids.append(DstId(rid=rid, pnc=pid))
-    g.remote_dma_fused([RemoteDMATransfer(dst_ids=ids, dma_engine_mask=m, remote_sem=rsem, srcs=[src],
-                                          dsts=[dst for _ in dsts])], local_sem=lsem)
-    return count(m)
+def plan(T, topo):
+    used, out = set(), []
+    place = lambda c: (topo.host(c), topo.chip(c))
+
+    def helper(s, hh, chip, same_die):
+        for h in range(512):
+            if (T.rank_of(h) is None and h not in used and (topo.host(h), topo.chip(h)) == (hh, chip)
+                    and (topo.die(h) == topo.die(s)) == same_die and topo.may_write(s, h)):
+                used.add(h)
+                return h
+        raise ValueError("no helper")
+
+    for s in T.cores:
+        hs, cs = place(s)
+        own = [d for d in T.cores if topo.host(d) == hs and d != s]
+        rack = [d for d in T.cores if topo.host(d) != hs and topo.rack(topo.host(d)) == topo.rack(hs)]
+        near = [d for d in T.cores if topo.rack(topo.host(d)) != topo.rack(hs) and topo.may_write(s, d)]
+        diag = [d for d in T.cores if topo.rack(topo.host(d)) != topo.rack(hs) and not topo.may_write(s, d)]
+        a = sorted(own + [s]).index(s)
+        if a == 1:
+            own = own[::-1]
+        turn = lambda v: [v[(a + k) % len(v)] for k in range(len(v))]
+        if near and diag:
+            m, z = turn(near), turn(diag)
+            hh = topo.host(m[0])
+            relays = [(helper(s, hh, cs, True), [m[0]], [z[1], z[2]]),
+                      (helper(s, hh, cs, False), [], [z[0]]),
+                      (helper(s, hs, cs, False), [], [m[1], m[2]])]
+            direct = own
+        elif near:
+            m, z = turn(near), turn(rack)
+            relays = [(helper(s, topo.host(m[0]), cs, False), [m[0]], [m[1], m[2]]),
+                      (helper(s, hs, cs, False), [], own),
+                      (helper(s, hs, cs, False), [], [z[0]])]
+            direct = [z[1], z[2]]
+        else:
+            m, z = turn(rack), turn(diag)
+            hh = [topo.host(h) for h in range(512) if topo.rack(topo.host(h)) != topo.rack(hs) and topo.may_write(s, h)][0]
+            relays = [(helper(s, hh, cs, True), [], [z[1], z[2]] if a != 1 else [z[2], z[1]]),
+                      (helper(s, topo.host(m[1]), topo.chip(m[1]), False), [m[1]], [d for d in z if topo.chip(d) == topo.chip(m[1])]),
+                      (helper(s, hs, cs, False), [], own),
+                      (helper(s, hs, cs, False), [], [m[0]])]
+            rest = [d for d in diag if d not in relays[1][2]]
+            relays[0] = (relays[0][0], [], rest if a != 1 else rest[::-1])
+            direct = [m[2]]
+        out.append((direct, relays))
+    return out
 
 
-def relay_program(g, core, T, topo, rank, n_in, dsts):
+def masks(topo, core, on, off):
+    moff = 0
+    for k, d in enumerate(off):
+        moff = topo.mask(core, d) & (moff if k else topo.mask(core, d))
+    mon = 0
+    for k, d in enumerate(on):
+        mon = topo.mask(core, d) & ~moff & (mon if k else topo.mask(core, d))
+    return mon, moff
+
+
+def links(topo, s, direct, relays):
+    here = lambda h: (topo.host(h), topo.chip(h)) == (topo.host(s), topo.chip(s))
+    on = [h for h, _, _ in relays if here(h)]
+    off = [h for h, _, _ in relays if not here(h)]
+    mon, moff = masks(topo, s, on, off + direct)
+    return on, off, mon, moff
+
+
+def send(g, topo, core, legs, src, dst, rsem, lsem):
+    n, tr = 0, []
+    for dsts, m in legs:
+        if not dsts:
+            continue
+        ids = []
+        for d in dsts:
+            rid, pid = topo.addr(d, core)
+            ids.append(DstId(rid=rid, pnc=pid))
+        tr.append(RemoteDMATransfer(dst_ids=ids, dma_engine_mask=m, remote_sem=rsem, srcs=[src], dsts=[dst for _ in dsts]))
+        n += count(m)
+    g.remote_dma_fused(tr, local_sem=lsem)
+    return n
+
+
+def helper_program(g, core, T, topo, rank, n_in, on, off):
     sem = T.sem
     lo = rank * W
+    mon, moff = masks(topo, core, on, off)
+    legs = [(off, moff), (on, mon)]
     g.wait_ge(sem.hc, n_in)
-    n = send(g, topo, core, dsts, T.hcnt[:], T.land[:, lo + CAP:lo + CAP + 2], sem.rcnt, sem.loc)
+    n = send(g, topo, core, legs, T.hcnt[:], T.land[:, lo + CAP:lo + CAP + 2], sem.rcnt, sem.loc)
     g.wait_ge(sem.hd, n_in)
-    n += send(g, topo, core, dsts, T.hdat[:], T.land[:, lo:lo + CAP], sem.rdat, sem.loc)
+    n += send(g, topo, core, legs, T.hdat[:], T.land[:, lo:lo + CAP], sem.rdat, sem.loc)
     g.wait_ge(sem.loc, n)
 
 
@@ -82,122 +127,160 @@ def rank_program(g, core, T, topo):
     rank = T.rank_of(core)
     if rank is None:
         for r, (direct, relays) in enumerate(routes):
-            for h, dsts in relays:
+            for h, on, off in relays:
                 if h == core:
-                    relay_program(g, core, T, topo, r, count(engines(topo, T.cores[r], [k for k, _ in relays])), dsts)
+                    hon, _, mon, moff = links(topo, T.cores[r], direct, relays)
+                    helper_program(g, core, T, topo, r, count(mon if h in hon else moff), on, off)
         return
     V, P, A, Y, sem = g.vector, g.tensor, g.scalar, g.sync, T.sem
     direct, relays = routes[rank]
     lo = rank * W
     loose = {"allow_small_or_imprecise_dtypes": True}
 
-    n_dir = sum(count(engines(topo, T.cores[r], routes[r][0])) for r in range(N) if core in routes[r][0])
-    n_rel = sum(count(engines(topo, h, dsts)) for _, rel in routes for h, dsts in rel if core in dsts)
+    n_dir = n_rel = 0
+    for r, (dr, rl) in enumerate(routes):
+        if core in dr:
+            n_dir += count(links(topo, T.cores[r], dr, rl)[3])
+        for h, on, off in rl:
+            mon, moff = masks(topo, h, on, off)
+            n_rel += count(mon) * (core in on) + count(moff) * (core in off)
 
     Y.dma_start(T.kb[:], T.keep[:]).then_inc(sem.ldk, 16)
     Y.dma_start(T.xs[:, 0:1024], T.x[:]).then_inc(sem.ldx, 16)
 
     g.iota(T.pint[:], [[128, 4]], 0, 1).then_inc(sem.i0, 1)
-    g.iota(T.jblk[:], [[1, 8], [0, 16]], 0, 0, **loose).then_inc(sem.i1, 1)
+    g.iota(T.U[:], [[64, 8], [1, 16]], 0, -1, **loose).then_inc(sem.i1, 1)
     g.iota(T.jrow[:], [[1, 128]], 0, 0, **loose).then_inc(sem.i2, 1)
     g.iota(T.jmod[:], [[0, 8], [1, 16]], 0, 0, **loose).then_inc(sem.i3, 1)
-    g.iota(T.k16f[:], [[16, K]], 0, 0, **loose).then_inc(sem.i4, 1)
-    hops = [h for h, _ in relays]
-    g.wait_ge(sem.scn, 1)
-    n_loc = send(g, topo, core, hops, T.land[:, lo + CAP:lo + CAP + 2], T.hcnt[:], sem.hc, sem.loc)
+    on, off, mon, moff = links(topo, core, direct, relays)
+    dat = T.land[:, lo:lo + CAP]
+    g.wait_ge(sem.sS, 1)
+    n_loc = send(g, topo, core, [(off, moff), (on, mon)], T.S[:, 64:66], T.hcnt[:], sem.hc, sem.loc)
     g.wait_ge(sem.sga, 1)
-    n_loc += send(g, topo, core, hops, T.land[:, lo:lo + CAP], T.hdat[:], sem.hd, sem.loc)
-    n_loc += send(g, topo, core, direct, T.land[:, lo:lo + CAP + 2], T.land[:, lo:lo + CAP + 2], sem.dir, sem.loc)
+    n_loc += send(g, topo, core, [(off[:1], moff), (on, mon)], dat, T.hdat[:], sem.hd, sem.loc)
+    for h in off[1:]:
+        n_loc += send(g, topo, core, [([h], moff)], dat, T.hdat[:], sem.hd, sem.loc)
+    g.wait_ge(sem.scn, 1)
+    n_loc += send(g, topo, core, [(direct, moff)], T.land[:, lo:lo + CAP + 2], T.land[:, lo:lo + CAP + 2], sem.dir, sem.loc)
     g.wait_ge(sem.loc, n_loc)
 
-    V.memset(T.ones[:], 1.0).then_inc(sem.mem, 1)
+    V.memset(T.S[:, 0:2], 0.0).then_inc(sem.mem, 1)
     V.memset(T.xs[:, 1024:1032], 0.0).then_inc(sem.mem, 1)
-    V.memset(T.cw[:, 64:72], 1000.0).then_inc(sem.mem, 1)
-    V.memset(T.land[:, END:END + 8], 0.0).then_inc(sem.mem, 1)
+    V.memset(T.selw[:], 0.0).then_inc(sem.mem, 1)
+    V.memset(T.ones[:], 1.0).then_inc(sem.mem, 1)
     V.wait_ge(sem.i0, 1)
-    V.tensor_scalar(T.pi2[:, 0:4], T.pint[:], 6, None, Op.arith_shift_right).then_inc(sem.pi, 1)
-    V.tensor_scalar(T.pi2[:, 4:5], T.pint[:, 0:1], 4, None, Op.arith_shift_right).then_inc(sem.pi, 1)
-    V.tensor_scalar(T.pi2[:, 5:6], T.pint[:, 0:1], 15, None, Op.bitwise_and).then_inc(sem.pi, 1)
-    V.tensor_copy(T.pf[:, 6:7], T.pint[:, 0:1]).then_inc(sem.pfs, 1)
-    V.wait_ge(sem.pi, 3)
-    V.tensor_copy(T.pf[:, 0:6], T.pi2[:]).then_inc(sem.pfs, 1)
-    V.wait_ge(sem.pfs, 2)
-    V.wait_ge(sem.i1, 1)
-    V.tensor_scalar(T.bo[:], T.jblk[:], T.pf[:, 4:5], None, Op.is_equal).then_inc(sem.sbo, 1)
-    for q in range(4):
-        V.tensor_scalar(T.selq[:, 128 * q:128 * q + 128], T.jblk[:], T.pf[:, q:q + 1], 16.0, Op.is_equal, Op.mult).then_inc(sem.ssel, 1)
-    V.wait_ge(sem.i2, 1)
-    V.tensor_scalar(T.lt[:], T.jrow[:], T.pf[:, 6:7], -1.0, Op.is_lt, Op.mult).then_inc(sem.slt, 1)
-    V.wait_ge(sem.sbo, 1)
-    V.wait_ge(sem.slt, 1)
-    V.tensor_tensor(T.ng[:], T.bo[:], T.lt[:], Op.mult).then_inc(sem.sng, 1)
-    V.wait_ge(sem.i3, 1)
-    V.tensor_scalar(T.hold[:], T.jmod[:], T.pf[:, 5:6], 4096.0, Op.is_equal, Op.mult).then_inc(sem.shd, 1)
-
+    p0 = T.pint[:, 0:1]
+    V.tensor_scalar(T.pi4[:, 0:1], p0, 4, None, Op.arith_shift_right).then_inc(sem.ph, 1)
+    V.tensor_scalar(T.pi4[:, 1:2], p0, 4, 1, Op.arith_shift_right, Op.bitwise_and).then_inc(sem.pp, 1)
+    V.tensor_scalar(T.pi4[:, 2:3], p0, 6, None, Op.arith_shift_right).then_inc(sem.p2, 1)
+    V.wait_ge(sem.ph, 1)
+    for k, b in enumerate((0.0, -7.5, 8.0)):
+        V.tensor_scalar(T.bias[:, k:k + 1], T.pi4[:, 0:1], -48.0, b, Op.mult, Op.add).then_inc(sem["bi%d" % k], 1)
+    V.wait_ge(sem.pp, 1)
+    V.tensor_scalar(T.pf[:, 0:1], T.pi4[:, 1:2], -1.0, 1.0, Op.mult, Op.add).then_inc(sem.pev, 1)
+    V.tensor_copy(T.pf[:, 1:2], T.pi4[:, 1:2]).then_inc(sem.pod, 1)
+    V.wait_ge(sem.p2, 1)
+    V.tensor_copy(T.pf[:, 2:3], T.pi4[:, 2:3]).then_inc(sem.p2f, 1)
+    V.wait_ge(sem.aab, 1)
+    V.tensor_scalar(T.bo[:], T.ab[:], 16.0, None, Op.is_le).then_inc(sem.sbo, 1)
+    V.wait_ge(sem.aal, 1)
+    V.tensor_scalar(T.le[:], T.al[:], 8.0, None, Op.is_le).then_inc(sem.sle, 1)
+    V.wait_ge(sem.aag, 1)
+    V.tensor_scalar(T.gt[:], T.ag[:], 7.5, None, Op.is_le).then_inc(sem.sgt, 1)
+    V.wait_ge(sem.pev, 1)
+    V.wait_ge(sem.pod, 1)
     V.wait_ge(sem.mem, 4)
+
     V.wait_ge(sem.ldk, 16)
-    V.tensor_copy(T.F[:], T.kb[:]).then_inc(sem.sF, 1)
-    V.wait_ge(sem.sF, 1)
-    V.tensor_tensor_scan(T.S[:], T.ones[:, 0:64], T.F[:], 0.0, Op.mult, Op.add).then_inc(sem.sS, 1)
+    V.tensor_scalar(T.FF[:, 1:65], T.kb[:], T.pf[:, 0:1], None, Op.mult).then_inc(sem.sff, 1)
+    V.tensor_scalar(T.FF[:, 65:129], T.kb[:], T.pf[:, 1:2], None, Op.mult).then_inc(sem.sff, 1)
+    V.wait_ge(sem.sff, 2)
+    V.tensor_tensor_scan(T.S[:, 2:66], T.FF[:, 1:65], T.FF[:, 65:129], 0.0, Op.add, Op.add).then_inc(sem.sS, 1)
+    V.wait_ge(sem.i2, 1)
+    V.wait_ge(sem.p2f, 1)
+    V.tensor_scalar(T.s1[:], T.jrow[:, 0:32], 16.0, T.pf[:, 2:3], Op.is_ge, Op.is_equal).then_inc(sem.ss1, 1)
+    V.wait_ge(sem.ss1, 1)
+    V.tensor_scalar(T.selw[:, 96:128], T.s1[:], 16.0, None, Op.mult).then_inc(sem.ssw, 1)
     V.wait_ge(sem.sbp, 2)
     for q in range(4):
         V.tensor_scalar(T.Z[:, 128 * q:128 * q + 128], T.jrow[:], T.pb[:, q:q + 1], None, Op.is_ge).then_inc(sem["z%d" % q], 1)
+    V.tensor_scalar(T.pi4[:, 3:4], p0, 15, None, Op.bitwise_and).then_inc(sem.pi, 1)
+    V.wait_ge(sem.spc, 1)
+    V.tensor_tensor(T.Z2[:], T.pc[:, 0:128], T.jrow[:], Op.is_le).then_inc(sem.sz2, 1)
+    V.wait_ge(sem.pi, 1)
+    V.tensor_copy(T.pf[:, 3:4], T.pi4[:, 3:4]).then_inc(sem.pif, 1)
+    V.wait_ge(sem.pif, 1)
+    V.wait_ge(sem.i3, 1)
+    V.tensor_scalar(T.hold[:], T.jmod[:], T.pf[:, 3:4], 4096.0, Op.is_equal, Op.mult).then_inc(sem.shd, 1)
     V.wait_ge(sem.shd, 1)
-    V.wait_ge(sem.sc1, 1)
-    V.tensor_tensor_scan(T.h1[:], T.hold[:], T.pc[:, 0:128], 0.0, Op.add, Op.min).then_inc(sem.sh1, 1)
-    V.wait_ge(sem.sh1, 1)
-    V.tensor_scalar(T.cl[:], T.h1[:, 15:128:16], 0.0625, None, Op.mult).then_inc(sem.scl, 1)
-    V.wait_ge(sem.scl, 1)
-    V.wait_ge(sem.scw, 1)
-    V.tensor_tensor(T.Z2[:], T.cw[:, 0:65].indirect(T.cl[:, 0:8]), T.jrow[:], Op.is_le).then_inc(sem.sz2, 1)
     V.wait_ge(sem.st1, 1)
     V.tensor_tensor_scan(T.h2[:], T.hold[:], T.pt[:, 0:128], 0.0, Op.add, Op.min).then_inc(sem.sh2, 1)
     V.wait_ge(sem.sh2, 1)
-    V.tensor_copy(T.tl[:], T.h2[:, 15:128:16]).then_inc(sem.stl, 1)
+    V.tensor_scalar(T.tl[:], T.h2[:, 15:128:16], -16.0, None, Op.add).then_inc(sem.stl, 1)
     V.wait_ge(sem.stl, 1)
     V.wait_ge(sem.ldx, 16)
     V.tensor_copy(T.land[:, lo:lo + CAP], T.xs[:, 0:1025].indirect(T.tl[:, 0:8])).then_inc(sem.sga, 1)
 
     P.wait_ge(sem.sbo, 1)
-    P.wait_ge(sem.sng, 1)
-    P.wait_ge(sem.sF, 1)
-    P.matmul(T.pcum[:, 0:64], T.ng[:], T.F[:], True, False)
+    P.wait_ge(sem.sle, 1)
+    P.wait_ge(sem.sgt, 1)
+    P.wait_ge(sem.sff, 2)
+    P.matmul(T.pd[:, 0:128], T.FF[:, 1:129], T.le[:], True, False)
+    P.wait_ge(sem.mem, 4)
     P.wait_ge(sem.sS, 1)
-    P.matmul(T.pb[0:64, 0:4], T.S[:], T.bo[:, 0:128:32], True, True).then_inc(sem.sbp, 1)
-    P.matmul(T.pb[64:128, 0:4], T.S[:], T.bo[:, 16:128:32], True, True).then_inc(sem.sbp, 1)
-    P.matmul(T.ptot[:, 0:2], T.bo[:], T.S[:, 62:64], True, True).then_inc(sem.stot, 1)
-    P.matmul(T.pcum[:, 0:64], T.bo[:], T.S[:], False, True).then_inc(sem.scum, 1)
-    P.wait_ge(sem.ssel, 4)
+    P.matmul(T.pb[0:64, 0:4], T.S[:, 1:65], T.bo[:, 0:128:32], True, True).then_inc(sem.sbp, 1)
+    P.matmul(T.pb[64:128, 0:4], T.S[:, 1:65], T.bo[:, 16:128:32], True, True).then_inc(sem.sbp, 1)
+    P.wait_ge(sem.sf0, 1)
+    P.matmul(T.pd[:, 0:128], T.FF[:, 0:128], T.gt[:], False, True).then_inc(sem.spd, 1)
+    P.wait_ge(sem.ssw, 1)
+
+    def block_number(q):
+        P.wait_ge(sem["z%d" % q], 1)
+        P.matmul(T.pt[:, 0:128], T.selw[:, 96 - 32 * q:224 - 32 * q], T.Z[:, 128 * q:128 * q + 128], q == 0, False)
+
+    block_number(0)
+    block_number(1)
+    P.wait_ge(sem.sdm, 1)
     for q in range(4):
         P.wait_ge(sem["z%d" % q], 1)
-        mm = P.matmul(T.pc[:, 0:128], T.selq[:, 128 * q:128 * q + 128], T.Z[:, 128 * q:128 * q + 128], q == 0, q == 3)
-    mm.then_inc(sem.sc1, 1)
-    for q in range(4):
-        P.matmul(T.pt[:, 0:128], T.selq[:, 128 * q:128 * q + 128], T.Z[:, 128 * q:128 * q + 128], q == 0, False)
+        mm = P.matmul(T.pc[32 * q:32 * q + 32, 0:128], T.dm[:, 32 * q:32 * q + 32], T.Z[:, 128 * q:128 * q + 128], True, True)
+    mm.then_inc(sem.spc, 1)
+    block_number(2)
+    block_number(3)
     P.wait_ge(sem.sz2, 1)
     P.matmul(T.pt[:, 0:128], T.bo[:], T.Z2[:], False, True).then_inc(sem.st1, 1)
 
-    A.wait_ge(sem.stot, 1)
-    A.activation(T.land[:, lo + CAP:lo + CAP + 2], T.ptot[:, 0:2], Act.Copy).then_inc(sem.scn, 1)
-    A.wait_ge(sem.scum, 1)
-    A.activation(T.cw[:, 0:64], T.pcum[:, 0:64], Act.Copy).then_inc(sem.scw, 1)
+    A.wait_ge(sem.i1, 1)
+    for k, (name, s) in enumerate((("ab", "aab"), ("al", "aal"), ("ag", "aag"))):
+        A.wait_ge(sem["bi%d" % k], 1)
+        A.activation(T[name][:] if False else {"ab": T.ab, "al": T.al, "ag": T.ag}[name][:], T.U[:], Act.Abs,
+                     T.bias[:, k:k + 1]).then_inc(sem[s], 1)
+    A.wait_ge(sem.sff, 2)
+    A.activation(T.FF[:, 0:1], T.FF[:, 64:65], Act.Copy, 0.0, -1.0).then_inc(sem.sf0, 1)
+    A.wait_ge(sem.spd, 1)
+    A.activation(T.dm[:], T.pd[:, 0:128], Act.Copy).then_inc(sem.sdm, 1)
+    A.wait_ge(sem.sS, 1)
+    A.activation(T.land[:, lo + CAP:lo + CAP + 2], T.S[:, 64:66], Act.Copy).then_inc(sem.scn, 1)
 
-    V.tensor_scalar(T.ident[:], T.jrow[:], T.pf[:, 6:7], None, Op.is_equal).then_inc(sem.sid, 1)
-    V.wait_ge(sem.i4, 1)
-    V.tensor_scalar(T.pos[:], T.k16f[:], T.pf[:, 5:6], None, Op.add).then_inc(sem.sps, 1)
-    V.tensor_copy(T.k16[:], T.k16f[:]).then_inc(sem.spm, 1)
-    V.tensor_scalar(T.pm[:], T.ones[:], T.pf[:, 5:6], None, Op.mult).then_inc(sem.spm, 1)
+    V.memset(T.land[:, END:END + 8], 0.0).then_inc(sem.mem, 1)
+    V.tensor_copy(T.pf[:, 4:5], p0).then_inc(sem.pfp, 1)
+    V.tensor_scalar(T.pos[:], T.jrow[:, 0:K], 16.0, T.pf[:, 3:4], Op.mult, Op.add).then_inc(sem.sps, 1)
+    V.tensor_scalar(T.k16[:], T.jrow[:, 0:K], 16.0, None, Op.mult).then_inc(sem.spm, 1)
+    V.tensor_scalar(T.pm[:], T.ones[:], T.pf[:, 3:4], None, Op.mult).then_inc(sem.spm, 1)
+    V.wait_ge(sem.pfp, 1)
+    V.tensor_scalar(T.ident[:], T.jrow[:], T.pf[:, 4:5], None, Op.is_equal).then_inc(sem.sid, 1)
     P.wait_ge(sem.sid, 1)
     P.wait_ge(sem.spm, 2)
     P.matmul(T.pl[:, 0:K], T.ident[:], T.k16[:], True, False)
     P.matmul(T.pl[:, 0:K], T.ident[:], T.pm[:], False, False)
+    P.wait_ge(sem.scn, 1)
+    P.wait_ge(sem.rcnt, n_rel)
+    P.wait_ge(sem.dir, n_dir)
+    P.matmul(T.pn[:, 0:N], T.bo[:], T.land[:, CAP + 1:END:W], True, True).then_inc(sem.spn, 1)
     V.wait_ge(sem.sps, 1)
-    V.wait_ge(sem.scn, 1)
-    V.wait_ge(sem.rcnt, n_rel)
-    V.wait_ge(sem.dir, n_dir)
-    cnts = T.land[:, CAP + 1:END:W]
-    V.tensor_tensor_scan(T.off[:], T.ones[:, 0:N], cnts, 0.0, Op.mult, Op.add).then_inc(sem.soff, 1)
-    V.tensor_scalar(T.dd[:], cnts, -1.0, float(W), Op.mult, Op.add).then_inc(sem.soff, 1)
+    V.wait_ge(sem.spn, 1)
+    V.tensor_tensor_scan(T.off[:], T.ones[:, 0:N], T.pn[:, 0:N], 0.0, Op.mult, Op.add).then_inc(sem.soff, 1)
+    V.tensor_scalar(T.dd[:], T.pn[:, 0:N], -1.0, float(W), Op.mult, Op.add).then_inc(sem.soff, 1)
     V.wait_ge(sem.soff, 2)
     for r in range(N):
         V.tensor_scalar(T.mr[:, K * r:K * r + K], T.pos[:], T.off[:, r:r + 1], T.dd[:, r:r + 1], Op.is_ge, Op.mult).then_inc(sem["m%d" % r], 1)
@@ -207,10 +290,14 @@ def rank_program(g, core, T, topo):
     V.wait_ge(sem.slp, 1)
     V.tensor_scalar(T.lst[:], T.pl[:, 0:K], float(END), None, Op.min).then_inc(sem.sls, 1)
 
+    V.wait_ge(sem.mem, 5)
+    A.wait_ge(sem.mem, 5)
     V.wait_ge(sem.sls, 1)
     A.wait_ge(sem.sls, 1)
-    V.wait_ge(sem.rdat, n_rel)
-    A.wait_ge(sem.rdat, n_rel)
+    for q in (V, A):
+        q.wait_ge(sem.sga, 1)
+        q.wait_ge(sem.dir, n_dir)
+        q.wait_ge(sem.rdat, n_rel)
     for k, (who, a, b) in enumerate(PIECES):
         win = T.land[:, 0:END + 1].indirect(T.lst[:, a:b])
         if who == "V":

from concourse.bass import DstId, RemoteDMATransfer
from concourse.mybir import AluOpType as Op, ActivationFunctionType as Act

N, CAP = 9, 128
W = 136
K = N * CAP // 16
END = N * W
PIECES = [("V", 0, 20), ("S", 36, 56), ("V", 20, 36), ("S", 56, 72)]

BF, F32, I32, U16 = "bfloat16", "float32", "int32", "uint16"
SB = {"kb": (64, I32), "xs": (1032, BF), "land": (END + 8, BF), "ysb": (N * CAP, BF), "hcnt": (2, BF), "hdat": (CAP, BF),
      "pint": (4, I32), "pi4": (4, I32), "pf": (8, F32), "bias": (4, F32), "ones": (72, BF), "U": (128, F32),
      "jrow": (128, BF), "jmod": (128, BF), "ab": (128, BF), "al": (128, BF), "ag": (128, BF), "bo": (128, BF),
      "le": (128, BF), "gt": (128, BF), "hold": (128, BF), "s1": (32, BF), "selw": (224, BF), "FF": (136, BF), "S": (72, BF),
      "dm": (128, BF), "Z": (512, BF), "Z2": (128, BF), "h2": (128, F32), "tl": (8, U16), "ident": (128, BF),
      "k16": (72, BF), "pm": (72, BF), "pos": (72, F32), "off": (N, F32), "dd": (N, F32), "mr": (N * 72, BF), "lst": (72, U16)}
SCRATCH = {k: ("sbuf", [128, n], t) for k, (n, t) in SB.items()}
for _k in ("pd", "pb", "pc", "pt", "pl", "pn"):
    SCRATCH[_k] = ("psum", [128, 512], F32)
SEMAPHORES = (["dir", "rcnt", "rdat", "hc", "hd", "loc", "ldk", "ldx", "i0", "i1", "i2", "i3", "mem", "ph", "pp", "pi", "p2",
               "pev", "pod", "pif", "p2f", "pfp", "bi0", "bi1", "bi2", "aab", "aal", "aag", "sbo", "sle", "sgt", "sff", "sf0",
               "sS", "ss1", "ssw", "shd", "sbp", "spd", "sdm", "spc", "sz2", "st1", "sh2", "stl", "sga", "scn", "sid", "spm",
               "sps", "spn", "soff", "slp", "sls", "sty", "sts"]
              + ["z%d" % q for q in range(4)] + ["m%d" % r for r in range(N)] + ["g%d" % k for k in range(4)])


def count(m):
    return bin(m).count("1")


def plan(T, topo):
    used, out = set(), []
    place = lambda c: (topo.host(c), topo.chip(c))

    def helper(s, hh, chip, same_die):
        for h in range(512):
            if (T.rank_of(h) is None and h not in used and (topo.host(h), topo.chip(h)) == (hh, chip)
                    and (topo.die(h) == topo.die(s)) == same_die and topo.may_write(s, h)):
                used.add(h)
                return h
        raise ValueError("no helper")

    for s in T.cores:
        hs, cs = place(s)
        own = [d for d in T.cores if topo.host(d) == hs and d != s]
        rack = [d for d in T.cores if topo.host(d) != hs and topo.rack(topo.host(d)) == topo.rack(hs)]
        near = [d for d in T.cores if topo.rack(topo.host(d)) != topo.rack(hs) and topo.may_write(s, d)]
        diag = [d for d in T.cores if topo.rack(topo.host(d)) != topo.rack(hs) and not topo.may_write(s, d)]
        a = sorted(own + [s]).index(s)
        if a == 1:
            own = own[::-1]
        turn = lambda v: [v[(a + k) % len(v)] for k in range(len(v))]
        if near and diag:
            m, z = turn(near), turn(diag)
            hh = topo.host(m[0])
            relays = [(helper(s, hh, cs, True), [m[0]], [z[1], z[2]]),
                      (helper(s, hh, cs, False), [], [z[0]]),
                      (helper(s, hs, cs, False), [], [m[1], m[2]])]
            direct = own
        elif near:
            m, z = turn(near), turn(rack)
            relays = [(helper(s, topo.host(m[0]), cs, False), [m[0]], [m[1], m[2]]),
                      (helper(s, hs, cs, False), [], own),
                      (helper(s, hs, cs, False), [], [z[0]])]
            direct = [z[1], z[2]]
        else:
            m, z = turn(rack), turn(diag)
            hh = [topo.host(h) for h in range(512) if topo.rack(topo.host(h)) != topo.rack(hs) and topo.may_write(s, h)][0]
            relays = [(helper(s, hh, cs, True), [], [z[1], z[2]] if a != 1 else [z[2], z[1]]),
                      (helper(s, topo.host(m[1]), topo.chip(m[1]), False), [m[1]], [d for d in z if topo.chip(d) == topo.chip(m[1])]),
                      (helper(s, hs, cs, False), [], own),
                      (helper(s, hs, cs, False), [], [m[0]])]
            rest = [d for d in diag if d not in relays[1][2]]
            relays[0] = (relays[0][0], [], rest if a != 1 else rest[::-1])
            direct = [m[2]]
        out.append((direct, relays))
    return out


def masks(topo, core, on, off):
    moff = 0
    for k, d in enumerate(off):
        moff = topo.mask(core, d) & (moff if k else topo.mask(core, d))
    mon = 0
    for k, d in enumerate(on):
        mon = topo.mask(core, d) & ~moff & (mon if k else topo.mask(core, d))
    return mon, moff


def links(topo, s, direct, relays):
    here = lambda h: (topo.host(h), topo.chip(h)) == (topo.host(s), topo.chip(s))
    on = [h for h, _, _ in relays if here(h)]
    off = [h for h, _, _ in relays if not here(h)]
    mon, moff = masks(topo, s, on, off + direct)
    return on, off, mon, moff


def send(g, topo, core, legs, src, dst, rsem, lsem):
    n, tr = 0, []
    for dsts, m in legs:
        if not dsts:
            continue
        ids = []
        for d in dsts:
            rid, pid = topo.addr(d, core)
            ids.append(DstId(rid=rid, pnc=pid))
        tr.append(RemoteDMATransfer(dst_ids=ids, dma_engine_mask=m, remote_sem=rsem, srcs=[src], dsts=[dst for _ in dsts]))
        n += count(m)
    g.remote_dma_fused(tr, local_sem=lsem)
    return n


def helper_program(g, core, T, topo, rank, n_in, on, off):
    sem = T.sem
    lo = rank * W
    mon, moff = masks(topo, core, on, off)
    legs = [(off, moff), (on, mon)]
    g.wait_ge(sem.hc, n_in)
    n = send(g, topo, core, legs, T.hcnt[:], T.land[:, lo + CAP:lo + CAP + 2], sem.rcnt, sem.loc)
    g.wait_ge(sem.hd, n_in)
    n += send(g, topo, core, legs, T.hdat[:], T.land[:, lo:lo + CAP], sem.rdat, sem.loc)
    g.wait_ge(sem.loc, n)


def rank_program(g, core, T, topo):
    routes = plan(T, topo)
    rank = T.rank_of(core)
    if rank is None:
        for r, (direct, relays) in enumerate(routes):
            for h, on, off in relays:
                if h == core:
                    hon, _, mon, moff = links(topo, T.cores[r], direct, relays)
                    helper_program(g, core, T, topo, r, count(mon if h in hon else moff), on, off)
        return
    V, P, A, Y, sem = g.vector, g.tensor, g.scalar, g.sync, T.sem
    direct, relays = routes[rank]
    lo = rank * W
    loose = {"allow_small_or_imprecise_dtypes": True}

    n_dir = n_rel = 0
    for r, (dr, rl) in enumerate(routes):
        if core in dr:
            n_dir += count(links(topo, T.cores[r], dr, rl)[3])
        for h, on, off in rl:
            mon, moff = masks(topo, h, on, off)
            n_rel += count(mon) * (core in on) + count(moff) * (core in off)

    Y.dma_start(T.kb[:], T.keep[:]).then_inc(sem.ldk, 16)
    Y.dma_start(T.xs[:, 0:1024], T.x[:]).then_inc(sem.ldx, 16)

    g.iota(T.pint[:], [[128, 4]], 0, 1).then_inc(sem.i0, 1)
    g.iota(T.U[:], [[64, 8], [1, 16]], 0, -1, **loose).then_inc(sem.i1, 1)
    g.iota(T.jrow[:], [[1, 128]], 0, 0, **loose).then_inc(sem.i2, 1)
    g.iota(T.jmod[:], [[0, 8], [1, 16]], 0, 0, **loose).then_inc(sem.i3, 1)
    on, off, mon, moff = links(topo, core, direct, relays)
    dat = T.land[:, lo:lo + CAP]
    g.wait_ge(sem.sS, 1)
    n_loc = send(g, topo, core, [(off, moff), (on, mon)], T.S[:, 64:66], T.hcnt[:], sem.hc, sem.loc)
    g.wait_ge(sem.sga, 1)
    n_loc += send(g, topo, core, [(off[:1], moff), (on, mon)], dat, T.hdat[:], sem.hd, sem.loc)
    for h in off[1:]:
        n_loc += send(g, topo, core, [([h], moff)], dat, T.hdat[:], sem.hd, sem.loc)
    g.wait_ge(sem.scn, 1)
    n_loc += send(g, topo, core, [(direct, moff)], T.land[:, lo:lo + CAP + 2], T.land[:, lo:lo + CAP + 2], sem.dir, sem.loc)
    g.wait_ge(sem.loc, n_loc)

    V.memset(T.S[:, 0:2], 0.0).then_inc(sem.mem, 1)
    V.memset(T.xs[:, 1024:1032], 0.0).then_inc(sem.mem, 1)
    V.memset(T.selw[:], 0.0).then_inc(sem.mem, 1)
    V.memset(T.ones[:], 1.0).then_inc(sem.mem, 1)
    V.wait_ge(sem.i0, 1)
    p0 = T.pint[:, 0:1]
    V.tensor_scalar(T.pi4[:, 0:1], p0, 4, None, Op.arith_shift_right).then_inc(sem.ph, 1)
    V.tensor_scalar(T.pi4[:, 1:2], p0, 4, 1, Op.arith_shift_right, Op.bitwise_and).then_inc(sem.pp, 1)
    V.tensor_scalar(T.pi4[:, 2:3], p0, 6, None, Op.arith_shift_right).then_inc(sem.p2, 1)
    V.wait_ge(sem.ph, 1)
    for k, b in enumerate((0.0, -7.5, 8.0)):
        V.tensor_scalar(T.bias[:, k:k + 1], T.pi4[:, 0:1], -48.0, b, Op.mult, Op.add).then_inc(sem["bi%d" % k], 1)
    V.wait_ge(sem.pp, 1)
    V.tensor_scalar(T.pf[:, 0:1], T.pi4[:, 1:2], -1.0, 1.0, Op.mult, Op.add).then_inc(sem.pev, 1)
    V.tensor_copy(T.pf[:, 1:2], T.pi4[:, 1:2]).then_inc(sem.pod, 1)
    V.wait_ge(sem.p2, 1)
    V.tensor_copy(T.pf[:, 2:3], T.pi4[:, 2:3]).then_inc(sem.p2f, 1)
    V.wait_ge(sem.aab, 1)
    V.tensor_scalar(T.bo[:], T.ab[:], 16.0, None, Op.is_le).then_inc(sem.sbo, 1)
    V.wait_ge(sem.aal, 1)
    V.tensor_scalar(T.le[:], T.al[:], 8.0, None, Op.is_le).then_inc(sem.sle, 1)
    V.wait_ge(sem.aag, 1)
    V.tensor_scalar(T.gt[:], T.ag[:], 7.5, None, Op.is_le).then_inc(sem.sgt, 1)
    V.wait_ge(sem.pev, 1)
    V.wait_ge(sem.pod, 1)
    V.wait_ge(sem.mem, 4)

    V.wait_ge(sem.ldk, 16)
    V.tensor_scalar(T.FF[:, 1:65], T.kb[:], T.pf[:, 0:1], None, Op.mult).then_inc(sem.sff, 1)
    V.tensor_scalar(T.FF[:, 65:129], T.kb[:], T.pf[:, 1:2], None, Op.mult).then_inc(sem.sff, 1)
    V.wait_ge(sem.sff, 2)
    V.tensor_tensor_scan(T.S[:, 2:66], T.FF[:, 1:65], T.FF[:, 65:129], 0.0, Op.add, Op.add).then_inc(sem.sS, 1)
    V.wait_ge(sem.i2, 1)
    V.wait_ge(sem.p2f, 1)
    V.tensor_scalar(T.s1[:], T.jrow[:, 0:32], 16.0, T.pf[:, 2:3], Op.is_ge, Op.is_equal).then_inc(sem.ss1, 1)
    V.wait_ge(sem.ss1, 1)
    V.tensor_scalar(T.selw[:, 96:128], T.s1[:], 16.0, None, Op.mult).then_inc(sem.ssw, 1)
    V.wait_ge(sem.sbp, 2)
    for q in range(4):
        V.tensor_scalar(T.Z[:, 128 * q:128 * q + 128], T.jrow[:], T.pb[:, q:q + 1], None, Op.is_ge).then_inc(sem["z%d" % q], 1)
    V.tensor_scalar(T.pi4[:, 3:4], p0, 15, None, Op.bitwise_and).then_inc(sem.pi, 1)
    V.wait_ge(sem.spc, 1)
    V.tensor_tensor(T.Z2[:], T.pc[:, 0:128], T.jrow[:], Op.is_le).then_inc(sem.sz2, 1)
    V.wait_ge(sem.pi, 1)
    V.tensor_copy(T.pf[:, 3:4], T.pi4[:, 3:4]).then_inc(sem.pif, 1)
    V.wait_ge(sem.pif, 1)
    V.wait_ge(sem.i3, 1)
    V.tensor_scalar(T.hold[:], T.jmod[:], T.pf[:, 3:4], 4096.0, Op.is_equal, Op.mult).then_inc(sem.shd, 1)
    V.wait_ge(sem.shd, 1)
    V.wait_ge(sem.st1, 1)
    V.tensor_tensor_scan(T.h2[:], T.hold[:], T.pt[:, 0:128], 0.0, Op.add, Op.min).then_inc(sem.sh2, 1)
    V.wait_ge(sem.sh2, 1)
    V.tensor_scalar(T.tl[:], T.h2[:, 15:128:16], -16.0, None, Op.add).then_inc(sem.stl, 1)
    V.wait_ge(sem.stl, 1)
    V.wait_ge(sem.ldx, 16)
    V.tensor_copy(T.land[:, lo:lo + CAP], T.xs[:, 0:1025].indirect(T.tl[:, 0:8])).then_inc(sem.sga, 1)

    P.wait_ge(sem.sbo, 1)
    P.wait_ge(sem.sle, 1)
    P.wait_ge(sem.sgt, 1)
    P.wait_ge(sem.sff, 2)
    P.matmul(T.pd[:, 0:128], T.FF[:, 1:129], T.le[:], True, False)
    P.wait_ge(sem.mem, 4)
    P.wait_ge(sem.sS, 1)
    P.matmul(T.pb[0:64, 0:4], T.S[:, 1:65], T.bo[:, 0:128:32], True, True).then_inc(sem.sbp, 1)
    P.matmul(T.pb[64:128, 0:4], T.S[:, 1:65], T.bo[:, 16:128:32], True, True).then_inc(sem.sbp, 1)
    P.wait_ge(sem.sf0, 1)
    P.matmul(T.pd[:, 0:128], T.FF[:, 0:128], T.gt[:], False, True).then_inc(sem.spd, 1)
    P.wait_ge(sem.ssw, 1)

    def block_number(q):
        P.wait_ge(sem["z%d" % q], 1)
        P.matmul(T.pt[:, 0:128], T.selw[:, 96 - 32 * q:224 - 32 * q], T.Z[:, 128 * q:128 * q + 128], q == 0, False)

    block_number(0)
    block_number(1)
    P.wait_ge(sem.sdm, 1)
    for q in range(4):
        P.wait_ge(sem["z%d" % q], 1)
        mm = P.matmul(T.pc[32 * q:32 * q + 32, 0:128], T.dm[:, 32 * q:32 * q + 32], T.Z[:, 128 * q:128 * q + 128], True, True)
    mm.then_inc(sem.spc, 1)
    block_number(2)
    block_number(3)
    P.wait_ge(sem.sz2, 1)
    P.matmul(T.pt[:, 0:128], T.bo[:], T.Z2[:], False, True).then_inc(sem.st1, 1)

    A.wait_ge(sem.i1, 1)
    for k, (name, s) in enumerate((("ab", "aab"), ("al", "aal"), ("ag", "aag"))):
        A.wait_ge(sem["bi%d" % k], 1)
        A.activation(T[name][:] if False else {"ab": T.ab, "al": T.al, "ag": T.ag}[name][:], T.U[:], Act.Abs,
                     T.bias[:, k:k + 1]).then_inc(sem[s], 1)
    A.wait_ge(sem.sff, 2)
    A.activation(T.FF[:, 0:1], T.FF[:, 64:65], Act.Copy, 0.0, -1.0).then_inc(sem.sf0, 1)
    A.wait_ge(sem.spd, 1)
    A.activation(T.dm[:], T.pd[:, 0:128], Act.Copy).then_inc(sem.sdm, 1)
    A.wait_ge(sem.sS, 1)
    A.activation(T.land[:, lo + CAP:lo + CAP + 2], T.S[:, 64:66], Act.Copy).then_inc(sem.scn, 1)

    V.memset(T.land[:, END:END + 8], 0.0).then_inc(sem.mem, 1)
    V.tensor_copy(T.pf[:, 4:5], p0).then_inc(sem.pfp, 1)
    V.tensor_scalar(T.pos[:], T.jrow[:, 0:K], 16.0, T.pf[:, 3:4], Op.mult, Op.add).then_inc(sem.sps, 1)
    V.tensor_scalar(T.k16[:], T.jrow[:, 0:K], 16.0, None, Op.mult).then_inc(sem.spm, 1)
    V.tensor_scalar(T.pm[:], T.ones[:], T.pf[:, 3:4], None, Op.mult).then_inc(sem.spm, 1)
    V.wait_ge(sem.pfp, 1)
    V.tensor_scalar(T.ident[:], T.jrow[:], T.pf[:, 4:5], None, Op.is_equal).then_inc(sem.sid, 1)
    P.wait_ge(sem.sid, 1)
    P.wait_ge(sem.spm, 2)
    P.matmul(T.pl[:, 0:K], T.ident[:], T.k16[:], True, False)
    P.matmul(T.pl[:, 0:K], T.ident[:], T.pm[:], False, False)
    P.wait_ge(sem.scn, 1)
    P.wait_ge(sem.rcnt, n_rel)
    P.wait_ge(sem.dir, n_dir)
    P.matmul(T.pn[:, 0:N], T.bo[:], T.land[:, CAP + 1:END:W], True, True).then_inc(sem.spn, 1)
    V.wait_ge(sem.sps, 1)
    V.wait_ge(sem.spn, 1)
    V.tensor_tensor_scan(T.off[:], T.ones[:, 0:N], T.pn[:, 0:N], 0.0, Op.mult, Op.add).then_inc(sem.soff, 1)
    V.tensor_scalar(T.dd[:], T.pn[:, 0:N], -1.0, float(W), Op.mult, Op.add).then_inc(sem.soff, 1)
    V.wait_ge(sem.soff, 2)
    for r in range(N):
        V.tensor_scalar(T.mr[:, K * r:K * r + K], T.pos[:], T.off[:, r:r + 1], T.dd[:, r:r + 1], Op.is_ge, Op.mult).then_inc(sem["m%d" % r], 1)
        P.wait_ge(sem["m%d" % r], 1)
        mm = P.matmul(T.pl[:, 0:K], T.ident[:], T.mr[:, K * r:K * r + K], False, r == N - 1)
    mm.then_inc(sem.slp, 1)
    V.wait_ge(sem.slp, 1)
    V.tensor_scalar(T.lst[:], T.pl[:, 0:K], float(END), None, Op.min).then_inc(sem.sls, 1)

    V.wait_ge(sem.mem, 5)
    A.wait_ge(sem.mem, 5)
    V.wait_ge(sem.sls, 1)
    A.wait_ge(sem.sls, 1)
    for q in (V, A):
        q.wait_ge(sem.sga, 1)
        q.wait_ge(sem.dir, n_dir)
        q.wait_ge(sem.rdat, n_rel)
    for k, (who, a, b) in enumerate(PIECES):
        win = T.land[:, 0:END + 1].indirect(T.lst[:, a:b])
        if who == "V":
            V.tensor_copy(T.ysb[:, 16 * a:16 * b], win).then_inc(sem["g%d" % k], 1)
        else:
            A.activation(T.ysb[:, 16 * a:16 * b], win, Act.Copy).then_inc(sem["g%d" % k], 1)
    for k, (who, a, b) in enumerate(PIECES[:3]):
        Y.wait_ge(sem["g%d" % k], 1)
        Y.dma_start(T.y[:, 16 * a:16 * b], T.ysb[:, 16 * a:16 * b]).then_inc(sem.sty, 16)
    a, b = PIECES[3][1:]
    A.wait_ge(sem.g3, 1)
    A.dma_start(T.y[:, 16 * a:16 * b], T.ysb[:, 16 * a:16 * b]).then_inc(sem.sts, 16)
    Y.wait_ge(sem.sty, 48)
    A.wait_ge(sem.sts, 16)
